import numpy as np
import ml_dtypes


def mxq(x, axis, fmt="e4m3"):
    dtype, down = {"e4m3": (ml_dtypes.float8_e4m3fn, 7), "e5m2": (ml_dtypes.float8_e5m2, 14)}[fmt]
    v = np.moveaxis(np.asarray(x, np.float32).astype(ml_dtypes.bfloat16).astype(np.float64), axis, -1)
    blocks = v.reshape(v.shape[:-1] + (-1, 32))
    amax = np.abs(blocks).max(-1, keepdims=True)
    byte = np.maximum(np.where(amax > 0, np.frexp(amax)[1] - 1 + 127, 0) - down, 1)
    scale = np.exp2(byte - 127.0)
    codes = (blocks / scale).astype(np.float32).astype(dtype).astype(np.float64)
    return np.moveaxis((codes * scale).reshape(v.shape), -1, axis)


WIDE = False


def mx_kscale(k, group=512):
    if not WIDE:
        return np.ones(k)
    levels = np.array([10, -10, 5, -5, 0])
    if group != 512:
        return np.exp2(np.random.permutation(np.resize(levels, k // group))).repeat(group)
    if k % 512:
        return np.exp2(np.random.permutation(np.resize(levels, k // 32))).repeat(32)
    a = np.empty((k // 512, 16))
    for p in range(k // 512):
        a[p, :8] = np.random.permutation(np.resize(levels, 8))
        for g in range(8):
            far = levels[np.abs(levels - a[p, g]) >= 10]
            a[p, g + 8] = far[np.random.randint(len(far))]
    return np.exp2(a.ravel()).repeat(32)


def f64(x):
    return np.asarray(x).astype(np.float64)


def striped(idx):
    return np.tile(np.asarray(idx).reshape(-1, 16).T, (8, 1)).astype(np.uint16)


def unstriped(offs):
    return offs[:16].T.reshape(-1).astype(np.int64)


H, KV, D, NQ, N = 4, 1, 256, 512, 512
CAP = 2.0


def setup_inputs():
    n = np.random.standard_normal
    s = mx_kscale(D, 0)[:, None]
    u = mx_kscale(N)
    t = np.random.uniform(0.5, 2.0, N) * u
    v = n((KV, N, 128))
    return {
        "qT": (n((H, D, NQ)) * s * (0.70 / np.sqrt(D))).astype(np.float32),
        "kT": (n((KV, D, N)) / s).astype(np.float32),
        "t": t.reshape(N, 1).astype(np.float32),
        "v": (v / t[:, None]).astype(np.float32),
        "kb": (0.5 * n((N, 1))).astype(np.float32),
        "og": n((H, NQ, 128)).astype(np.float32),
    }


def reference(qT, kT, t, v, kb, og):
    a = np.repeat(mxq(f64(kT), 1, "e4m3"), H // KV, 0).transpose(0, 2, 1) @ mxq(f64(qT), 1, "e4m3")
    a = a + f64(kb)
    a = CAP * np.tanh(a / CAP)
    p = np.maximum(a, 0.0)
    w = p * f64(t)
    y = mxq(w, 1, "e4m3").transpose(0, 2, 1) @ np.repeat(mxq(f64(v), 1, "e4m3"), H // KV, 0)
    y = y / 16.0
    y = y / (1.0 + np.exp(-f64(og)))
    return y

@@ -1,0 +1,214 @@
+from contextlib import ExitStack
+
+import concourse.mybir as mybir
+
+H, D, NQ, N, E = 4, 256, 512, 512, 128
+CAP = 2.0
+FLOPS = 2 * H * NQ * N * (D + E)
+
+F32 = mybir.dt.float32
+BF16 = mybir.dt.bfloat16
+U32 = mybir.dt.uint32
+U8 = mybir.dt.uint8
+FP8X4 = mybir.dt.float8_e4m3fn_x4
+ACT = mybir.ActivationFunctionType
+ALU = mybir.AluOpType
+
+P = 128
+PACK = 4
+ROWS = 64
+COLS = 128
+PAD = 17
+CHUNKS = [(0,0,128),(0,128,128),(0,256,256),(1,0,256),(1,256,128),(1,384,128)]
+ORDER = "iv0 qq0 ik0 ik1 qk0 qk1 qk2 qk3 ik2 ik3 qk4 qk5 qk6 qk7 mm0 mm1 th0 th1 iv1 vi0 qq1 mm2 mm3 vq0 ww0 th2 is2 ww1 qw0 qq2 th3 mm4 gg0 ww2 qw1 fi0 th4 mm5 ww3 qw2 fi1 is3 ww4 qw3 fi2 qq3 th5 mm6 gg1 mm7 th6 ww5 qw4 fi3 is4 th7 ww6 qw5 qq4 mm8 mm9 fi4 gg2 is5 th8 ww7 qw6 qq5 mm10 fi5 th9 mm11 gg3 th10 ww8 qw7 fi6 th11 ww9 qw8 fi7 ww10 qw9 fi8 ww11 qw10 fi9 qw11 fi10 fi11".split()
+
+
+def tile_rows_a_relu_kb_cap_gate_kernel(tc, qT, kT, t, v, kb, og, out):
+    nc = tc.nc
+    with ExitStack() as ctx:
+        sb = ctx.enter_context(tc.tile_pool(name="sb", bufs=1))
+        ps = ctx.enter_context(tc.psum_pool(name="ps", bufs=1))
+        ctx.enter_context(tc.manual_schedule())
+
+        def mx_tiles(name, width):
+            grouped = sb.tile([P, width * PACK], BF16, name=name + "_g", align_bytes=64)
+            codes = sb.tile([P, width], U32, name=name + "_c", align_bytes=64)
+            scales = sb.tile([P, width], U8, name=name + "_s", align_bytes=64)
+            return grouped, codes, scales
+
+        def quantize(grouped, codes, scales):
+            nc.vector.quantize_mx(out=codes.bitcast(FP8X4), scales=scales, in_=grouped)
+
+        def interleave(engine, grouped, raw):
+            dst = grouped.rearrange("p (c i j) -> p c j i", i=4, j=PACK)
+            src = raw.rearrange("p j (c i) -> p c j i", i=4)
+            if engine == "v":
+                nc.vector.tensor_copy(out=dst, in_=src)
+            else:
+                nc.scalar.copy(out=dst, in_=src)
+
+        score_banks = [[ps.tile([P, 512], F32, name="sc%d_%d" % (g, b)) for b in range(3)] for g in range(2)]
+        y_banks = [ps.tile([P, 512], F32, name="y%d" % b) for b in range(2)]
+
+        k_raw = [sb.tile([P, PACK, 256], F32, name="k_raw%d" % a, align_bytes=64) for a in range(2)]
+        k_g = [[sb.tile([P, 2, 64, PACK], BF16, name="k_g%d_%d" % (a, b), align_bytes=64) for b in range(2)] for a in range(2)]
+        k_c = sb.tile([P, PACK, COLS], U32, name="k_c", align_bytes=64)
+        k_s = sb.tile([P, PACK, COLS], U8, name="k_s", align_bytes=64)
+        v_raw = sb.tile([P, PACK, E], F32, name="v_raw", align_bytes=64)
+        v_mx = mx_tiles("v", E)
+        t_raw = sb.tile([P, PACK], F32, name="t_raw")
+        kb_raw = sb.tile([P, PACK], F32, name="kb_raw")
+        t_cap = sb.tile([P, PACK], F32, name="t_cap")
+        kb_cap = sb.tile([P, PACK], F32, name="kb_cap")
+        warm = sb.tile([P, 1], F32, name="warm")
+        warm2 = sb.tile([P, 1], F32, name="warm2")
+        q_raw = [sb.tile([P, PACK, c[2]], F32, name="q_raw%d" % i, align_bytes=64) for i, c in enumerate(CHUNKS)]
+        q_mx = [mx_tiles("q%d" % i, c[2]) for i, c in enumerate(CHUNKS)]
+        og_raw = [sb.tile([P, 2, 2, E], F32, name="og_raw%d" % i, align_bytes=64) for i in range(4)]
+        gate = [sb.tile([P, 2, 2, E], F32, name="gate%d" % i, align_bytes=64) for i in range(4)]
+        units = [(i, g) for i in range(len(CHUNKS)) for g in range(2)]
+        th = [sb.tile([P, PACK * (CHUNKS[i][2] + PAD)], F32, name="th%d" % u, align_bytes=64) for u, (i, g) in enumerate(units)]
+        w_mx = [mx_tiles("w%d" % u, CHUNKS[i][2]) for u, (i, g) in enumerate(units)]
+        res = [sb.tile([P, CHUNKS[i][2]], F32, name="res%d" % u, align_bytes=64) for u, (i, g) in enumerate(units)]
+
+        banks_of = []
+        turn = [0, 0]
+        for i, g in units:
+            nb = CHUNKS[i][2] * PACK // 512
+            banks_of.append([score_banks[g][(sum(CHUNKS[a][2] for a in range(i)) * PACK // 512 + b) % 3] for b in range(nb)])
+
+        def score_view(u, r):
+            nq = CHUNKS[units[u][0]][2]
+            per = 512 // nq
+            return banks_of[u][r // per][:, (r % per) * nq : (r % per + 1) * nq]
+
+        def load_q(i):
+            pair, q0, nq = CHUNKS[i]
+            nc.sync.dma_start(out=q_raw[i][:], in_=qT[2 * pair : 2 * pair + 2, :, q0 : q0 + nq].rearrange("g (p j) n -> (g p) j n", j=PACK))
+
+        def load_k(a, g, engine):
+            engine.dma_start(out=k_raw[a][ROWS * g : ROWS * (g + 1)], in_=kT[0, :, 256 * a : 256 * (a + 1)].rearrange("(p j) n -> p j n", j=PACK))
+
+        def load_og(i):
+            pair, half = divmod(i, 2)
+            for g in range(2):
+                nc.sync.dma_start(out=og_raw[i][:, g], in_=og[2 * pair + g, 256 * half : 256 * (half + 1), :].rearrange("(c p) e -> p c e", p=P))
+
+        def interleave_k(a, b):
+            dst = k_g[a][b][:].rearrange("p r s j -> p s r j")
+            src = k_raw[a][:].rearrange("p j (s r) -> p s r j", r=PACK)[:, :, 2 * b : 2 * b + 2, :]
+            if b == 0:
+                nc.vector.tensor_copy(out=dst, in_=src)
+            else:
+                nc.scalar.copy(out=dst, in_=src)
+
+        def quantize_k(a, r):
+            cols = slice(64 * a, 64 * (a + 1))
+            quantize(k_g[a][r // 2][:, r % 2].rearrange("p s j -> p (s j)"), k_c[:, r, cols], k_s[:, r, cols])
+
+        def scores(u):
+            i, g = units[u]
+            rows = slice(ROWS * g, ROWS * (g + 1))
+            for r in range(PACK):
+                for c0 in range(0, CHUNKS[i][2], COLS):
+                    cols = slice(c0, c0 + COLS)
+                    nc.tensor.matmul_mx(
+                        out=score_view(u, r)[:, cols],
+                        lhsT=k_c[rows, r, :].bitcast(FP8X4),
+                        lhsT_scale=k_s[rows, r, :],
+                        rhs=q_mx[i][1][rows, cols].bitcast(FP8X4),
+                        rhs_scale=q_mx[i][2][rows, cols],
+                        start=True,
+                        stop=True,
+                    )
+
+        def th_view(u):
+            nq = CHUNKS[units[u][0]][2]
+            return th[u][:].rearrange("p (r c) -> p r c", r=PACK)[:, :, 0:nq]
+
+        def cap(u):
+            for r in range(PACK):
+                nc.scalar.activation(out=th_view(u)[:, r, :], in_=score_view(u, r), func=ACT.Tanh, bias=kb_cap[:, r : r + 1], scale=1.0 / CAP)
+
+        def weigh(u):
+            nq = CHUNKS[units[u][0]][2]
+            nc.vector.scalar_tensor_tensor(
+                out=w_mx[u][0][:].rearrange("p (c r) -> p c r", r=PACK),
+                in0=th_view(u).rearrange("p r c -> p c r"),
+                scalar=0.0,
+                in1=t_cap[:].unsqueeze(1).to_broadcast([P, nq, PACK]),
+                op0=ALU.max,
+                op1=ALU.mult,
+            )
+
+        def values(u):
+            nq = CHUNKS[units[u][0]][2]
+            for c0 in range(0, nq, COLS):
+                cols = slice(c0, c0 + COLS)
+                nc.tensor.matmul_mx(
+                    out=y_banks[u % 2][:, cols],
+                    lhsT=w_mx[u][1][:, cols].bitcast(FP8X4),
+                    lhsT_scale=w_mx[u][2][:, cols],
+                    rhs=v_mx[1][:].bitcast(FP8X4),
+                    rhs_scale=v_mx[2][:],
+                    start=True,
+                    stop=True,
+                )
+
+        def finish(u):
+            i, g = units[u]
+            pair, q0, nq = CHUNKS[i]
+            half, rest = divmod(q0, 256)
+            gv = gate[2 * pair + half][:, g].rearrange("p c e -> p (c e)")[:, rest : rest + nq]
+            nc.vector.scalar_tensor_tensor(out=res[u][:], in0=y_banks[u % 2][:, 0:nq], scalar=1.0 / 16.0, in1=gv, op0=ALU.mult, op1=ALU.mult)
+            nc.sync.dma_start(
+                out=out[2 * pair + g, q0 : q0 + nq, :].rearrange("(c p) e -> p c e", p=P),
+                in_=res[u][:].rearrange("p (c e) -> p c e", e=E),
+            )
+
+        load_q(0)
+        load_k(0, 0, nc.sync)
+        load_k(0, 1, nc.scalar)
+        load_k(1, 0, nc.sync)
+        load_k(1, 1, nc.scalar)
+        nc.scalar.dma_start(out=kb_raw[:], in_=kb.rearrange("(p j) o -> p (j o)", j=PACK))
+        nc.scalar.dma_start(out=t_raw[:], in_=t.rearrange("(p j) o -> p (j o)", j=PACK))
+        nc.gpsimd.memset(warm[:], 0.0)
+        nc.scalar.activation(out=warm2[:], in_=warm[:], func=ACT.Sigmoid)
+        for name in "q1 v o0 q2 o1 q3 q4 q5 o2 o3".split():
+            if name == "v":
+                nc.sync.dma_start(out=v_raw[:], in_=v[0].rearrange("(p j) e -> p j e", j=PACK))
+            elif name[0] == "q":
+                load_q(int(name[1:]))
+            else:
+                load_og(int(name[1:]))
+        nc.gpsimd.tensor_scalar(out=kb_cap[:], in0=kb_raw[:], scalar1=1.0 / CAP, scalar2=0.0, op0=ALU.mult, op1=ALU.add)
+        nc.gpsimd.tensor_scalar(out=t_cap[:], in0=t_raw[:], scalar1=CAP, scalar2=0.0, op0=ALU.mult, op1=ALU.add)
+
+        for step in ORDER:
+            kind, n = step[0:2], int(step[2:])
+            if kind == "iv" or kind == "is":
+                interleave(kind[1], q_mx[n][0][:], q_raw[n][:])
+            elif kind == "qq":
+                quantize(q_mx[n][0][:], q_mx[n][1][:], q_mx[n][2][:])
+            elif kind == "ik":
+                interleave_k(n // 2, n % 2)
+            elif kind == "qk":
+                quantize_k(n // 4, n % 4)
+            elif kind == "vi":
+                interleave("v" if n == 0 else "s", v_mx[0][:], v_raw[:])
+            elif kind == "vq":
+                quantize(v_mx[0][:], v_mx[1][:], v_mx[2][:])
+            elif kind == "mm":
+                scores(n)
+            elif kind == "th":
+                cap(n)
+            elif kind == "ww":
+                weigh(n)
+            elif kind == "qw":
+                quantize(w_mx[n][0][:], w_mx[n][1][:], w_mx[n][2][:])
+                values(n)
+            elif kind == "gg":
+                nc.scalar.activation(out=gate[n][:], in_=og_raw[n][:], func=ACT.Sigmoid)
+            else:
+                finish(n)

@@ -4,6 +4,7 @@ import concourse.mybir as mybir
 
 H, D, NQ, N, E = 4, 256, 512, 512, 128
 CAP = 2.0
+Y_SCALE = 1.0 / 16.0
 FLOPS = 2 * H * NQ * N * (D + E)
 
 F32 = mybir.dt.float32
@@ -16,199 +17,249 @@ ALU = mybir.AluOpType
 
 P = 128
 PACK = 4
-ROWS = 64
+ROWS = D // PACK
+PAIR = P // ROWS
 COLS = 128
-PAD = 17
-CHUNKS = [(0,0,128),(0,128,128),(0,256,256),(1,0,256),(1,256,128),(1,384,128)]
-ORDER = "iv0 qq0 ik0 ik1 qk0 qk1 qk2 qk3 ik2 ik3 qk4 qk5 qk6 qk7 mm0 mm1 th0 th1 iv1 vi0 qq1 mm2 mm3 vq0 ww0 th2 is2 ww1 qw0 qq2 th3 mm4 gg0 ww2 qw1 fi0 th4 mm5 ww3 qw2 fi1 is3 ww4 qw3 fi2 qq3 th5 mm6 gg1 mm7 th6 ww5 qw4 fi3 is4 th7 ww6 qw5 qq4 mm8 mm9 fi4 gg2 is5 th8 ww7 qw6 qq5 mm10 fi5 th9 mm11 gg3 th10 ww8 qw7 fi6 th11 ww9 qw8 fi7 ww10 qw9 fi8 ww11 qw10 fi9 qw11 fi10 fi11".split()
+BANK = 512
+CHUNK = 256
+CHUNKS = (H // PAIR) * (NQ // CHUNK)
+SLOTS = BANK // CHUNK
+SCORE_BANKS = 3
+HALF = N // 2
+NEAR = 4
+
+LOADS = "q1 v0 q2 o0 q3 o1 o2 o3".split()
+
+ORDER = """
+qi0 qq0 ki0 ki1 kq0 kq1 kq2 kq3 ki2 ki3 kq4 kq5 sc0 kq6 kq7 tk0 sc1 qi1 th0 th1
+vi0 th2 qq1 vq0 we0 qi2 th3 sc2 sc3 th4 th5 th6 we1 qq2 iw0 qi3 sc4 th7 wq0 qq3
+th8 we2 ga0 sc5 th9 th10 we3 th11 we4 iw1 we5 sc6 pv0 th12 th13 fi0 sc7 wq1 is2 th14
+pv1 iv2 wh12 wh13 th15 wq2 wh14 wh15 ga1 pv2 iv3 ga2 fi1 hq6 is3 fi2 hp6 ga3 hq7 hf6
+hp7 hf7
+""".split()
 
 
 def tile_rows_a_relu_kb_cap_gate_kernel(tc, qT, kT, t, v, kb, og, out):
     nc = tc.nc
     with ExitStack() as ctx:
-        sb = ctx.enter_context(tc.tile_pool(name="sb", bufs=1))
-        ps = ctx.enter_context(tc.psum_pool(name="ps", bufs=1))
+        sbuf = ctx.enter_context(tc.tile_pool(name="sbuf", bufs=1))
+        psum = ctx.enter_context(tc.psum_pool(name="psum", bufs=1))
         ctx.enter_context(tc.manual_schedule())
 
-        def mx_tiles(name, width):
-            grouped = sb.tile([P, width * PACK], BF16, name=name + "_g", align_bytes=64)
-            codes = sb.tile([P, width], U32, name=name + "_c", align_bytes=64)
-            scales = sb.tile([P, width], U8, name=name + "_s", align_bytes=64)
-            return grouped, codes, scales
+        def tiles(name, count, shape, dtype):
+            return [sbuf.tile(shape, dtype, name="%s%d" % (name, n), align_bytes=64) for n in range(count)]
 
-        def quantize(grouped, codes, scales):
-            nc.vector.quantize_mx(out=codes.bitcast(FP8X4), scales=scales, in_=grouped)
+        score_banks = [[psum.tile([P, BANK], F32, name="score%d_%d" % (g, b)) for b in range(SCORE_BANKS)] for g in range(PAIR)]
+        y_banks = [psum.tile([P, BANK], F32, name="y%d" % b) for b in range(2)]
 
-        def interleave(engine, grouped, raw):
-            dst = grouped.rearrange("p (c i j) -> p c j i", i=4, j=PACK)
-            src = raw.rearrange("p j (c i) -> p c j i", i=4)
-            if engine == "v":
+        k_rows = tiles("k_rows", 2, [P, PACK, HALF], F32)
+        k_words = tiles("k_words", 4, [P, 2, HALF // PACK, PACK], BF16)
+        k_codes = tiles("k_codes", 1, [P, PACK, COLS], U32)[0]
+        k_scales = tiles("k_scales", 1, [P, PACK, COLS], U8)[0]
+        v_rows = tiles("v_rows", 1, [P, PACK, E], F32)[0]
+        v_words = tiles("v_words", 1, [P, E * PACK], BF16)[0]
+        v_codes = tiles("v_codes", 1, [P, E], U32)[0]
+        v_scales = tiles("v_scales", 1, [P, E], U8)[0]
+        q_rows = tiles("q_rows", CHUNKS, [P, PACK, CHUNK], F32)
+        q_words = tiles("q_words", CHUNKS, [P, CHUNK * PACK], BF16)
+        q_codes = tiles("q_codes", CHUNKS, [P, CHUNK], U32)
+        q_scales = tiles("q_scales", CHUNKS, [P, CHUNK], U8)
+        capped = tiles("capped", CHUNKS, [P, PACK, PAIR * CHUNK], F32)
+        w_rows = tiles("w_rows", CHUNKS, [P, PACK, PAIR * CHUNK], BF16)
+        w_words = tiles("w_words", CHUNKS, [P, PAIR * CHUNK * PACK], BF16)
+        w_codes = tiles("w_codes", CHUNKS, [P, PAIR * CHUNK], U32)
+        w_scales = tiles("w_scales", CHUNKS, [P, PAIR * CHUNK], U8)
+        og_raw = tiles("og_raw", CHUNKS, [P, PAIR * CHUNK], F32)
+        gate = tiles("gate", CHUNKS, [P, PAIR * CHUNK], F32)
+        result = tiles("result", CHUNKS, [P, PAIR * CHUNK], F32)
+        kb_raw, t_raw, kb_over_cap, t_times_cap = tiles("token", 4, [P, PACK], F32)
+        table_in, table_out = tiles("table", 2, [P, 1], F32)
+
+        def chunk_heads(chunk):
+            pair = chunk // (NQ // CHUNK)
+            return slice(PAIR * pair, PAIR * (pair + 1))
+
+        def chunk_queries(chunk):
+            first = CHUNK * (chunk % (NQ // CHUNK))
+            return slice(first, first + CHUNK)
+
+        def head_columns(heads, scale=1):
+            return slice(heads.start * CHUNK * scale, heads.stop * CHUNK * scale)
+
+        def by_query_pairs(tensor, chunk, heads):
+            first = chunk_heads(chunk).start
+            return tensor[first + heads.start : first + heads.stop, chunk_queries(chunk), :].rearrange("g (m c) e -> m g (c e)", c=2)
+
+        def copy(on_vector, dst, src):
+            if on_vector:
                 nc.vector.tensor_copy(out=dst, in_=src)
             else:
                 nc.scalar.copy(out=dst, in_=src)
 
-        score_banks = [[ps.tile([P, 512], F32, name="sc%d_%d" % (g, b)) for b in range(3)] for g in range(2)]
-        y_banks = [ps.tile([P, 512], F32, name="y%d" % b) for b in range(2)]
-
-        k_raw = [sb.tile([P, PACK, 256], F32, name="k_raw%d" % a, align_bytes=64) for a in range(2)]
-        k_g = [[sb.tile([P, 2, 64, PACK], BF16, name="k_g%d_%d" % (a, b), align_bytes=64) for b in range(2)] for a in range(2)]
-        k_c = sb.tile([P, PACK, COLS], U32, name="k_c", align_bytes=64)
-        k_s = sb.tile([P, PACK, COLS], U8, name="k_s", align_bytes=64)
-        v_raw = sb.tile([P, PACK, E], F32, name="v_raw", align_bytes=64)
-        v_mx = mx_tiles("v", E)
-        t_raw = sb.tile([P, PACK], F32, name="t_raw")
-        kb_raw = sb.tile([P, PACK], F32, name="kb_raw")
-        t_cap = sb.tile([P, PACK], F32, name="t_cap")
-        kb_cap = sb.tile([P, PACK], F32, name="kb_cap")
-        warm = sb.tile([P, 1], F32, name="warm")
-        warm2 = sb.tile([P, 1], F32, name="warm2")
-        q_raw = [sb.tile([P, PACK, c[2]], F32, name="q_raw%d" % i, align_bytes=64) for i, c in enumerate(CHUNKS)]
-        q_mx = [mx_tiles("q%d" % i, c[2]) for i, c in enumerate(CHUNKS)]
-        og_raw = [sb.tile([P, 2, 2, E], F32, name="og_raw%d" % i, align_bytes=64) for i in range(4)]
-        gate = [sb.tile([P, 2, 2, E], F32, name="gate%d" % i, align_bytes=64) for i in range(4)]
-        units = [(i, g) for i in range(len(CHUNKS)) for g in range(2)]
-        th = [sb.tile([P, PACK * (CHUNKS[i][2] + PAD)], F32, name="th%d" % u, align_bytes=64) for u, (i, g) in enumerate(units)]
-        w_mx = [mx_tiles("w%d" % u, CHUNKS[i][2]) for u, (i, g) in enumerate(units)]
-        res = [sb.tile([P, CHUNKS[i][2]], F32, name="res%d" % u, align_bytes=64) for u, (i, g) in enumerate(units)]
-
-        banks_of = []
-        turn = [0, 0]
-        for i, g in units:
-            nb = CHUNKS[i][2] * PACK // 512
-            banks_of.append([score_banks[g][(sum(CHUNKS[a][2] for a in range(i)) * PACK // 512 + b) % 3] for b in range(nb)])
-
-        def score_view(u, r):
-            nq = CHUNKS[units[u][0]][2]
-            per = 512 // nq
-            return banks_of[u][r // per][:, (r % per) * nq : (r % per + 1) * nq]
-
-        def load_q(i):
-            pair, q0, nq = CHUNKS[i]
-            nc.sync.dma_start(out=q_raw[i][:], in_=qT[2 * pair : 2 * pair + 2, :, q0 : q0 + nq].rearrange("g (p j) n -> (g p) j n", j=PACK))
-
-        def load_k(a, g, engine):
-            engine.dma_start(out=k_raw[a][ROWS * g : ROWS * (g + 1)], in_=kT[0, :, 256 * a : 256 * (a + 1)].rearrange("(p j) n -> p j n", j=PACK))
-
-        def load_og(i):
-            pair, half = divmod(i, 2)
-            for g in range(2):
-                nc.sync.dma_start(out=og_raw[i][:, g], in_=og[2 * pair + g, 256 * half : 256 * (half + 1), :].rearrange("(c p) e -> p c e", p=P))
-
-        def interleave_k(a, b):
-            dst = k_g[a][b][:].rearrange("p r s j -> p s r j")
-            src = k_raw[a][:].rearrange("p j (s r) -> p s r j", r=PACK)[:, :, 2 * b : 2 * b + 2, :]
-            if b == 0:
-                nc.vector.tensor_copy(out=dst, in_=src)
-            else:
-                nc.scalar.copy(out=dst, in_=src)
-
-        def quantize_k(a, r):
-            cols = slice(64 * a, 64 * (a + 1))
-            quantize(k_g[a][r // 2][:, r % 2].rearrange("p s j -> p (s j)"), k_c[:, r, cols], k_s[:, r, cols])
-
-        def scores(u):
-            i, g = units[u]
-            rows = slice(ROWS * g, ROWS * (g + 1))
-            for r in range(PACK):
-                for c0 in range(0, CHUNKS[i][2], COLS):
-                    cols = slice(c0, c0 + COLS)
-                    nc.tensor.matmul_mx(
-                        out=score_view(u, r)[:, cols],
-                        lhsT=k_c[rows, r, :].bitcast(FP8X4),
-                        lhsT_scale=k_s[rows, r, :],
-                        rhs=q_mx[i][1][rows, cols].bitcast(FP8X4),
-                        rhs_scale=q_mx[i][2][rows, cols],
-                        start=True,
-                        stop=True,
-                    )
-
-        def th_view(u):
-            nq = CHUNKS[units[u][0]][2]
-            return th[u][:].rearrange("p (r c) -> p r c", r=PACK)[:, :, 0:nq]
-
-        def cap(u):
-            for r in range(PACK):
-                nc.scalar.activation(out=th_view(u)[:, r, :], in_=score_view(u, r), func=ACT.Tanh, bias=kb_cap[:, r : r + 1], scale=1.0 / CAP)
-
-        def weigh(u):
-            nq = CHUNKS[units[u][0]][2]
-            nc.vector.scalar_tensor_tensor(
-                out=w_mx[u][0][:].rearrange("p (c r) -> p c r", r=PACK),
-                in0=th_view(u).rearrange("p r c -> p c r"),
-                scalar=0.0,
-                in1=t_cap[:].unsqueeze(1).to_broadcast([P, nq, PACK]),
-                op0=ALU.max,
-                op1=ALU.mult,
+        def interleave(on_vector, words, rows):
+            copy(
+                on_vector,
+                words.rearrange("p (c i j) -> p c j i", i=NEAR, j=PACK),
+                rows.rearrange("p j (c i) -> p c j i", i=NEAR),
             )
 
-        def values(u):
-            nq = CHUNKS[units[u][0]][2]
-            for c0 in range(0, nq, COLS):
-                cols = slice(c0, c0 + COLS)
-                nc.tensor.matmul_mx(
-                    out=y_banks[u % 2][:, cols],
-                    lhsT=w_mx[u][1][:, cols].bitcast(FP8X4),
-                    lhsT_scale=w_mx[u][2][:, cols],
-                    rhs=v_mx[1][:].bitcast(FP8X4),
-                    rhs_scale=v_mx[2][:],
-                    start=True,
-                    stop=True,
+        def quantize(words, codes, scales):
+            nc.vector.quantize_mx(out=codes.bitcast(FP8X4), scales=scales, in_=words)
+
+        def matmul(dst, lhs_codes, lhs_scales, rhs_codes, rhs_scales):
+            nc.tensor.matmul_mx(
+                out=dst,
+                lhsT=lhs_codes.bitcast(FP8X4),
+                lhsT_scale=lhs_scales,
+                rhs=rhs_codes.bitcast(FP8X4),
+                rhs_scale=rhs_scales,
+                start=True,
+                stop=True,
+            )
+
+        def load_queries(chunk):
+            src = qT[chunk_heads(chunk), :, chunk_queries(chunk)].rearrange("g (p j) n -> (g p) j n", j=PACK)
+            nc.sync.dma_start(out=q_rows[chunk][:], in_=src)
+
+        def interleave_keys(half, part):
+            src = k_rows[half][:].rearrange("p j (s r) -> p s r j", r=PACK)[:, :, 2 * part : 2 * part + 2, :]
+            copy(part == 0, k_words[2 * half + part][:].rearrange("p r s j -> p s r j"), src)
+
+        def quantize_keys(half, slot):
+            cols = slice(half * HALF // PACK, (half + 1) * HALF // PACK)
+            words = k_words[2 * half + slot // 2][:, slot % 2].rearrange("p s j -> p (s j)")
+            quantize(words, k_codes[:, slot, cols], k_scales[:, slot, cols])
+
+        def scale_token_columns():
+            nc.vector.tensor_scalar_mul(out=kb_over_cap[:], in0=kb_raw[:], scalar1=1.0 / CAP)
+            nc.vector.tensor_scalar_mul(out=t_times_cap[:], in0=t_raw[:], scalar1=CAP)
+
+        def step_slots(step):
+            first = SLOTS * (step % (PACK // SLOTS))
+            return range(first, first + SLOTS)
+
+        def score_columns(step, g, slot):
+            first = (slot % SLOTS) * CHUNK
+            return score_banks[g][step % SCORE_BANKS][:, first : first + CHUNK]
+
+        def scores(step):
+            chunk = step // (PACK // SLOTS)
+            for slot in step_slots(step):
+                for first in range(0, CHUNK, COLS):
+                    cols = slice(first, first + COLS)
+                    for g in range(PAIR):
+                        rows = slice(ROWS * g, ROWS * (g + 1))
+                        matmul(
+                            score_columns(step, g, slot)[:, cols],
+                            k_codes[rows, slot, :],
+                            k_scales[rows, slot, :],
+                            q_codes[chunk][rows, cols],
+                            q_scales[chunk][rows, cols],
+                        )
+
+        def cap(step, g):
+            chunk = step // (PACK // SLOTS)
+            for slot in step_slots(step):
+                nc.scalar.activation(
+                    out=capped[chunk][:, slot, head_columns(range(g, g + 1))].rearrange("p (c m) -> p c m", c=2),
+                    in_=score_columns(step, g, slot).rearrange("p (m c) -> p c m", c=2),
+                    func=ACT.Tanh,
+                    bias=kb_over_cap[:, slot : slot + 1],
+                    scale=1.0 / CAP,
                 )
 
-        def finish(u):
-            i, g = units[u]
-            pair, q0, nq = CHUNKS[i]
-            half, rest = divmod(q0, 256)
-            gv = gate[2 * pair + half][:, g].rearrange("p c e -> p (c e)")[:, rest : rest + nq]
-            nc.vector.scalar_tensor_tensor(out=res[u][:], in0=y_banks[u % 2][:, 0:nq], scalar=1.0 / 16.0, in1=gv, op0=ALU.mult, op1=ALU.mult)
-            nc.sync.dma_start(
-                out=out[2 * pair + g, q0 : q0 + nq, :].rearrange("(c p) e -> p c e", p=P),
-                in_=res[u][:].rearrange("p (c e) -> p c e", e=E),
+        def weigh(step, heads):
+            chunk = step // (PACK // SLOTS)
+            for slot in step_slots(step):
+                nc.vector.tensor_scalar(
+                    out=w_rows[chunk][:, slot, head_columns(heads)],
+                    in0=capped[chunk][:, slot, head_columns(heads)],
+                    scalar1=0.0,
+                    scalar2=t_times_cap[:, slot : slot + 1],
+                    op0=ALU.max,
+                    op1=ALU.mult,
+                )
+
+        def interleave_weights(on_vector, chunk, heads):
+            interleave(on_vector, w_words[chunk][:, head_columns(heads, PACK)], w_rows[chunk][:, :, head_columns(heads)])
+
+        def quantize_weights(chunk, heads):
+            cols = head_columns(heads)
+            quantize(w_words[chunk][:, head_columns(heads, PACK)], w_codes[chunk][:, cols], w_scales[chunk][:, cols])
+
+        def y_columns(chunk, heads):
+            return y_banks[(chunk + heads.start) % 2][:, 0 : len(heads) * CHUNK]
+
+        def multiply_values(chunk, heads):
+            for first in range(0, len(heads) * CHUNK, COLS):
+                cols = slice(heads.start * CHUNK + first, heads.start * CHUNK + first + COLS)
+                matmul(
+                    y_columns(chunk, heads)[:, first : first + COLS],
+                    w_codes[chunk][:, cols],
+                    w_scales[chunk][:, cols],
+                    v_codes[:],
+                    v_scales[:],
+                )
+
+        def finish(chunk, heads):
+            cols = head_columns(heads)
+            nc.vector.scalar_tensor_tensor(
+                out=result[chunk][:, cols],
+                in0=y_columns(chunk, heads),
+                scalar=Y_SCALE,
+                in1=gate[chunk][:, cols],
+                op0=ALU.mult,
+                op1=ALU.mult,
             )
+            src = result[chunk][:, cols].rearrange("p (g x) -> p g x", x=CHUNK)
+            nc.sync.dma_start(out=by_query_pairs(out, chunk, heads), in_=src)
 
-        load_q(0)
-        load_k(0, 0, nc.sync)
-        load_k(0, 1, nc.scalar)
-        load_k(1, 0, nc.sync)
-        load_k(1, 1, nc.scalar)
-        nc.scalar.dma_start(out=kb_raw[:], in_=kb.rearrange("(p j) o -> p (j o)", j=PACK))
-        nc.scalar.dma_start(out=t_raw[:], in_=t.rearrange("(p j) o -> p (j o)", j=PACK))
-        nc.gpsimd.memset(warm[:], 0.0)
-        nc.scalar.activation(out=warm2[:], in_=warm[:], func=ACT.Sigmoid)
-        for name in "q1 v o0 q2 o1 q3 q4 q5 o2 o3".split():
-            if name == "v":
-                nc.sync.dma_start(out=v_raw[:], in_=v[0].rearrange("(p j) e -> p j e", j=PACK))
-            elif name[0] == "q":
-                load_q(int(name[1:]))
-            else:
-                load_og(int(name[1:]))
-        nc.gpsimd.tensor_scalar(out=kb_cap[:], in0=kb_raw[:], scalar1=1.0 / CAP, scalar2=0.0, op0=ALU.mult, op1=ALU.add)
-        nc.gpsimd.tensor_scalar(out=t_cap[:], in0=t_raw[:], scalar1=CAP, scalar2=0.0, op0=ALU.mult, op1=ALU.add)
+        both = range(PAIR)
 
-        for step in ORDER:
-            kind, n = step[0:2], int(step[2:])
-            if kind == "iv" or kind == "is":
-                interleave(kind[1], q_mx[n][0][:], q_raw[n][:])
-            elif kind == "qq":
-                quantize(q_mx[n][0][:], q_mx[n][1][:], q_mx[n][2][:])
-            elif kind == "ik":
-                interleave_k(n // 2, n % 2)
-            elif kind == "qk":
-                quantize_k(n // 4, n % 4)
-            elif kind == "vi":
-                interleave("v" if n == 0 else "s", v_mx[0][:], v_raw[:])
-            elif kind == "vq":
-                quantize(v_mx[0][:], v_mx[1][:], v_mx[2][:])
-            elif kind == "mm":
-                scores(n)
-            elif kind == "th":
-                cap(n)
-            elif kind == "ww":
-                weigh(n)
-            elif kind == "qw":
-                quantize(w_mx[n][0][:], w_mx[n][1][:], w_mx[n][2][:])
-                values(n)
-            elif kind == "gg":
-                nc.scalar.activation(out=gate[n][:], in_=og_raw[n][:], func=ACT.Sigmoid)
+        load_queries(0)
+        for half in range(2):
+            src = kT[0, :, half * HALF : (half + 1) * HALF].rearrange("(p j) n -> p j n", j=PACK)
+            nc.sync.dma_start(out=k_rows[half][0:ROWS], in_=src)
+            nc.scalar.dma_start(out=k_rows[half][ROWS:P], in_=src)
+        nc.scalar.dma_start(out=kb_raw[:], in_=kb.rearrange("(s r) o -> s (r o)", r=PACK))
+        nc.scalar.dma_start(out=t_raw[:], in_=t.rearrange("(s r) o -> s (r o)", r=PACK))
+        nc.vector.memset(table_in[:], 0.0)
+        nc.scalar.activation(out=table_out[:], in_=table_in[:], func=ACT.Sigmoid)
+        for name in LOADS:
+            n = int(name[1:])
+            if name[0] == "q":
+                load_queries(n)
+            elif name[0] == "v":
+                nc.sync.dma_start(out=v_rows[:], in_=v[n].rearrange("(s r) e -> s r e", r=PACK))
             else:
-                finish(n)
+                dst = og_raw[n][:].rearrange("p (g x) -> p g x", x=CHUNK)
+                nc.sync.dma_start(out=dst, in_=by_query_pairs(og, n, both))
+
+        def one(n):
+            return n // PAIR, range(n % PAIR, n % PAIR + 1)
+
+        stages = {
+            "qi": lambda n: interleave(True, q_words[n][:], q_rows[n][:]),
+            "qq": lambda n: quantize(q_words[n][:], q_codes[n][:], q_scales[n][:]),
+            "vi": lambda n: interleave(True, v_words[:], v_rows[:]),
+            "vq": lambda n: quantize(v_words[:], v_codes[:], v_scales[:]),
+            "ki": lambda n: interleave_keys(*divmod(n, 2)),
+            "kq": lambda n: quantize_keys(*divmod(n, PACK)),
+            "tk": lambda n: scale_token_columns(),
+            "sc": scores,
+            "th": lambda n: cap(*divmod(n, PAIR)),
+            "we": lambda n: weigh(n, both),
+            "wh": lambda n: weigh(*one(n)),
+            "iw": lambda n: interleave_weights(True, n, both),
+            "iv": lambda n: interleave_weights(True, n, range(0, 1)),
+            "is": lambda n: interleave_weights(False, n, range(1, 2)),
+            "ga": lambda n: nc.scalar.activation(out=gate[n][:], in_=og_raw[n][:], func=ACT.Sigmoid),
+            "wq": lambda n: quantize_weights(n, both),
+            "pv": lambda n: multiply_values(n, both),
+            "fi": lambda n: finish(n, both),
+            "hq": lambda n: quantize_weights(*one(n)),
+            "hp": lambda n: multiply_values(*one(n)),
+            "hf": lambda n: finish(*one(n)),
+        }
+        for name in ORDER:
+            stages[name[0:2]](int(name[2:]))

from contextlib import ExitStack

import concourse.mybir as mybir

H, D, NQ, N, E = 4, 256, 512, 512, 128
CAP = 2.0
Y_SCALE = 1.0 / 16.0
FLOPS = 2 * H * NQ * N * (D + E)

F32 = mybir.dt.float32
BF16 = mybir.dt.bfloat16
U32 = mybir.dt.uint32
U8 = mybir.dt.uint8
FP8X4 = mybir.dt.float8_e4m3fn_x4
ACT = mybir.ActivationFunctionType
ALU = mybir.AluOpType

P = 128
PACK = 4
ROWS = D // PACK
PAIR = P // ROWS
COLS = 128
BANK = 512
CHUNK = 256
CHUNKS = (H // PAIR) * (NQ // CHUNK)
SLOTS = BANK // CHUNK
SCORE_BANKS = 3
HALF = N // 2
NEAR = 4

LOADS = "q1 v0 q2 o0 q3 o1 o2 o3".split()

ORDER = """
qi0 qq0 ki0 ki1 kq0 kq1 kq2 kq3 ki2 ki3 kq4 kq5 sc0 kq6 kq7 tk0 sc1 qi1 th0 th1
vi0 th2 qq1 vq0 we0 qi2 th3 sc2 sc3 th4 th5 th6 we1 qq2 iw0 qi3 sc4 th7 wq0 qq3
th8 we2 ga0 sc5 th9 th10 we3 th11 we4 iw1 we5 sc6 pv0 th12 th13 fi0 sc7 wq1 is2 th14
pv1 iv2 wh12 wh13 th15 wq2 wh14 wh15 ga1 pv2 iv3 ga2 fi1 hq6 is3 fi2 hp6 ga3 hq7 hf6
hp7 hf7
""".split()


def tile_rows_a_relu_kb_cap_gate_kernel(tc, qT, kT, t, v, kb, og, out):
    nc = tc.nc
    with ExitStack() as ctx:
        sbuf = ctx.enter_context(tc.tile_pool(name="sbuf", bufs=1))
        psum = ctx.enter_context(tc.psum_pool(name="psum", bufs=1))
        ctx.enter_context(tc.manual_schedule())

        def tiles(name, count, shape, dtype):
            return [sbuf.tile(shape, dtype, name="%s%d" % (name, n), align_bytes=64) for n in range(count)]

        score_banks = [[psum.tile([P, BANK], F32, name="score%d_%d" % (g, b)) for b in range(SCORE_BANKS)] for g in range(PAIR)]
        y_banks = [psum.tile([P, BANK], F32, name="y%d" % b) for b in range(2)]

        k_rows = tiles("k_rows", 2, [P, PACK, HALF], F32)
        k_words = tiles("k_words", 4, [P, 2, HALF // PACK, PACK], BF16)
        k_codes = tiles("k_codes", 1, [P, PACK, COLS], U32)[0]
        k_scales = tiles("k_scales", 1, [P, PACK, COLS], U8)[0]
        v_rows = tiles("v_rows", 1, [P, PACK, E], F32)[0]
        v_words = tiles("v_words", 1, [P, E * PACK], BF16)[0]
        v_codes = tiles("v_codes", 1, [P, E], U32)[0]
        v_scales = tiles("v_scales", 1, [P, E], U8)[0]
        q_rows = tiles("q_rows", CHUNKS, [P, PACK, CHUNK], F32)
        q_words = tiles("q_words", CHUNKS, [P, CHUNK * PACK], BF16)
        q_codes = tiles("q_codes", CHUNKS, [P, CHUNK], U32)
        q_scales = tiles("q_scales", CHUNKS, [P, CHUNK], U8)
        capped = tiles("capped", CHUNKS, [P, PACK, PAIR * CHUNK], F32)
        w_rows = tiles("w_rows", CHUNKS, [P, PACK, PAIR * CHUNK], BF16)
        w_words = tiles("w_words", CHUNKS, [P, PAIR * CHUNK * PACK], BF16)
        w_codes = tiles("w_codes", CHUNKS, [P, PAIR * CHUNK], U32)
        w_scales = tiles("w_scales", CHUNKS, [P, PAIR * CHUNK], U8)
        og_raw = tiles("og_raw", CHUNKS, [P, PAIR * CHUNK], F32)
        gate = tiles("gate", CHUNKS, [P, PAIR * CHUNK], F32)
        result = tiles("result", CHUNKS, [P, PAIR * CHUNK], F32)
        kb_raw, t_raw, kb_over_cap, t_times_cap = tiles("token", 4, [P, PACK], F32)
        table_in, table_out = tiles("table", 2, [P, 1], F32)

        def chunk_heads(chunk):
            pair = chunk // (NQ // CHUNK)
            return slice(PAIR * pair, PAIR * (pair + 1))

        def chunk_queries(chunk):
            first = CHUNK * (chunk % (NQ // CHUNK))
            return slice(first, first + CHUNK)

        def head_columns(heads, scale=1):
            return slice(heads.start * CHUNK * scale, heads.stop * CHUNK * scale)

        def by_query_pairs(tensor, chunk, heads):
            first = chunk_heads(chunk).start
            return tensor[first + heads.start : first + heads.stop, chunk_queries(chunk), :].rearrange("g (m c) e -> m g (c e)", c=2)

        def copy(on_vector, dst, src):
            if on_vector:
                nc.vector.tensor_copy(out=dst, in_=src)
            else:
                nc.scalar.copy(out=dst, in_=src)

        def interleave(on_vector, words, rows):
            copy(
                on_vector,
                words.rearrange("p (c i j) -> p c j i", i=NEAR, j=PACK),
                rows.rearrange("p j (c i) -> p c j i", i=NEAR),
            )

        def quantize(words, codes, scales):
            nc.vector.quantize_mx(out=codes.bitcast(FP8X4), scales=scales, in_=words)

        def matmul(dst, lhs_codes, lhs_scales, rhs_codes, rhs_scales):
            nc.tensor.matmul_mx(
                out=dst,
                lhsT=lhs_codes.bitcast(FP8X4),
                lhsT_scale=lhs_scales,
                rhs=rhs_codes.bitcast(FP8X4),
                rhs_scale=rhs_scales,
                start=True,
                stop=True,
            )

        def load_queries(chunk):
            src = qT[chunk_heads(chunk), :, chunk_queries(chunk)].rearrange("g (p j) n -> (g p) j n", j=PACK)
            nc.sync.dma_start(out=q_rows[chunk][:], in_=src)

        def interleave_keys(half, part):
            src = k_rows[half][:].rearrange("p j (s r) -> p s r j", r=PACK)[:, :, 2 * part : 2 * part + 2, :]
            copy(part == 0, k_words[2 * half + part][:].rearrange("p r s j -> p s r j"), src)

        def quantize_keys(half, slot):
            cols = slice(half * HALF // PACK, (half + 1) * HALF // PACK)
            words = k_words[2 * half + slot // 2][:, slot % 2].rearrange("p s j -> p (s j)")
            quantize(words, k_codes[:, slot, cols], k_scales[:, slot, cols])

        def scale_token_columns():
            nc.vector.tensor_scalar_mul(out=kb_over_cap[:], in0=kb_raw[:], scalar1=1.0 / CAP)
            nc.vector.tensor_scalar_mul(out=t_times_cap[:], in0=t_raw[:], scalar1=CAP)

        def step_slots(step):
            first = SLOTS * (step % (PACK // SLOTS))
            return range(first, first + SLOTS)

        def score_columns(step, g, slot):
            first = (slot % SLOTS) * CHUNK
            return score_banks[g][step % SCORE_BANKS][:, first : first + CHUNK]

        def scores(step):
            chunk = step // (PACK // SLOTS)
            for slot in step_slots(step):
                for first in range(0, CHUNK, COLS):
                    cols = slice(first, first + COLS)
                    for g in range(PAIR):
                        rows = slice(ROWS * g, ROWS * (g + 1))
                        matmul(
                            score_columns(step, g, slot)[:, cols],
                            k_codes[rows, slot, :],
                            k_scales[rows, slot, :],
                            q_codes[chunk][rows, cols],
                            q_scales[chunk][rows, cols],
                        )

        def cap(step, g):
            chunk = step // (PACK // SLOTS)
            for slot in step_slots(step):
                nc.scalar.activation(
                    out=capped[chunk][:, slot, head_columns(range(g, g + 1))].rearrange("p (c m) -> p c m", c=2),
                    in_=score_columns(step, g, slot).rearrange("p (m c) -> p c m", c=2),
                    func=ACT.Tanh,
                    bias=kb_over_cap[:, slot : slot + 1],
                    scale=1.0 / CAP,
                )

        def weigh(step, heads):
            chunk = step // (PACK // SLOTS)
            for slot in step_slots(step):
                nc.vector.tensor_scalar(
                    out=w_rows[chunk][:, slot, head_columns(heads)],
                    in0=capped[chunk][:, slot, head_columns(heads)],
                    scalar1=0.0,
                    scalar2=t_times_cap[:, slot : slot + 1],
                    op0=ALU.max,
                    op1=ALU.mult,
                )

        def interleave_weights(on_vector, chunk, heads):
            interleave(on_vector, w_words[chunk][:, head_columns(heads, PACK)], w_rows[chunk][:, :, head_columns(heads)])

        def quantize_weights(chunk, heads):
            cols = head_columns(heads)
            quantize(w_words[chunk][:, head_columns(heads, PACK)], w_codes[chunk][:, cols], w_scales[chunk][:, cols])

        def y_columns(chunk, heads):
            return y_banks[(chunk + heads.start) % 2][:, 0 : len(heads) * CHUNK]

        def multiply_values(chunk, heads):
            for first in range(0, len(heads) * CHUNK, COLS):
                cols = slice(heads.start * CHUNK + first, heads.start * CHUNK + first + COLS)
                matmul(
                    y_columns(chunk, heads)[:, first : first + COLS],
                    w_codes[chunk][:, cols],
                    w_scales[chunk][:, cols],
                    v_codes[:],
                    v_scales[:],
                )

        def finish(chunk, heads):
            cols = head_columns(heads)
            nc.vector.scalar_tensor_tensor(
                out=result[chunk][:, cols],
                in0=y_columns(chunk, heads),
                scalar=Y_SCALE,
                in1=gate[chunk][:, cols],
                op0=ALU.mult,
                op1=ALU.mult,
            )
            src = result[chunk][:, cols].rearrange("p (g x) -> p g x", x=CHUNK)
            nc.sync.dma_start(out=by_query_pairs(out, chunk, heads), in_=src)

        both = range(PAIR)

        load_queries(0)
        for half in range(2):
            src = kT[0, :, half * HALF : (half + 1) * HALF].rearrange("(p j) n -> p j n", j=PACK)
            nc.sync.dma_start(out=k_rows[half][0:ROWS], in_=src)
            nc.scalar.dma_start(out=k_rows[half][ROWS:P], in_=src)
        nc.scalar.dma_start(out=kb_raw[:], in_=kb.rearrange("(s r) o -> s (r o)", r=PACK))
        nc.scalar.dma_start(out=t_raw[:], in_=t.rearrange("(s r) o -> s (r o)", r=PACK))
        nc.vector.memset(table_in[:], 0.0)
        nc.scalar.activation(out=table_out[:], in_=table_in[:], func=ACT.Sigmoid)
        for name in LOADS:
            n = int(name[1:])
            if name[0] == "q":
                load_queries(n)
            elif name[0] == "v":
                nc.sync.dma_start(out=v_rows[:], in_=v[n].rearrange("(s r) e -> s r e", r=PACK))
            else:
                dst = og_raw[n][:].rearrange("p (g x) -> p g x", x=CHUNK)
                nc.sync.dma_start(out=dst, in_=by_query_pairs(og, n, both))

        def one(n):
            return n // PAIR, range(n % PAIR, n % PAIR + 1)

        stages = {
            "qi": lambda n: interleave(True, q_words[n][:], q_rows[n][:]),
            "qq": lambda n: quantize(q_words[n][:], q_codes[n][:], q_scales[n][:]),
            "vi": lambda n: interleave(True, v_words[:], v_rows[:]),
            "vq": lambda n: quantize(v_words[:], v_codes[:], v_scales[:]),
            "ki": lambda n: interleave_keys(*divmod(n, 2)),
            "kq": lambda n: quantize_keys(*divmod(n, PACK)),
            "tk": lambda n: scale_token_columns(),
            "sc": scores,
            "th": lambda n: cap(*divmod(n, PAIR)),
            "we": lambda n: weigh(n, both),
            "wh": lambda n: weigh(*one(n)),
            "iw": lambda n: interleave_weights(True, n, both),
            "iv": lambda n: interleave_weights(True, n, range(0, 1)),
            "is": lambda n: interleave_weights(False, n, range(1, 2)),
            "ga": lambda n: nc.scalar.activation(out=gate[n][:], in_=og_raw[n][:], func=ACT.Sigmoid),
            "wq": lambda n: quantize_weights(n, both),
            "pv": lambda n: multiply_values(n, both),
            "fi": lambda n: finish(n, both),
            "hq": lambda n: quantize_weights(*one(n)),
            "hp": lambda n: multiply_values(*one(n)),
            "hf": lambda n: finish(*one(n)),
        }
        for name in ORDER:
            stages[name[0:2]](int(name[2:]))
